import numpy as np, ml_dtypes
CORES = [23,119,17,113]
N = 4
BF = ml_dtypes.bfloat16
def gentries(a):
    return np.ascontiguousarray(a.reshape(8, 16, -1).transpose(0, 2, 1)).reshape(8, -1)
def gtable(e):
    e = np.asarray(e); return np.ascontiguousarray(e.reshape(8, -1, 16).transpose(0, 2, 1)).reshape(128, -1).astype(np.int32)
def f(rng, *shape):
    return (rng.standard_normal(shape, dtype=np.float32) * np.exp2(rng.integers(-2, 3, shape[:-1] + (1,)))).astype(BF)
def wide(rng, *shape):
    v = f(rng, *shape).astype(np.float32); k = shape[:-2] + (1, shape[-1])
    return (v * np.exp2(rng.integers(-6, 7, k)) * (rng.random(k) > 0.0625)).astype(BF)
W, C, D, B, R, K = 8192, 1536, 4, 3, 10, 1000
def ints(x):
    return np.clip(np.rint(x), -32768, 32768).astype(BF)
def cols(fr, ix):
    return np.take_along_axis(fr.reshape(N, 8, 16, W), ix[None, :, None, :], 3).astype(np.float32).astype(np.int64)
def limits(rng, fr):
    m = 512; lim = np.zeros((8, 16, D), np.int64); s = cols(fr, rng.integers(0, W, (8, m)))
    for l in range(D):
        s = s + cols(fr, rng.integers(0, W, (8, m))); en = np.sum(np.abs(s), axis=(0, 2)); o = np.argsort(en, axis=1)
        lim[:, :, l] = np.take_along_axis(np.take_along_axis(en, o, 1), rng.integers(m // 5, 4 * m // 5, (8, 16)), 1)
        s = np.take_along_axis(s, o[:, rng.integers(0, m // 2, m)][None, :, None, :], 3)
    return lim
def parts(rng):
    fr = ints(f(rng, N, 128, W).astype(np.float32) * 1024)
    return fr, rng.integers(0, W, (8, W)), rng.integers(0, W, (8, C))
def pack(fr, first, start, lim):
    return {"frag": fr, "first": np.stack([first.astype(np.int32)] * N), "start": np.stack([gtable(start)] * N), "lim": np.stack([lim.reshape(128, D).astype(np.int32)] * N)}
def setup_inputs(rng):
    fr, first, start = parts(rng)
    return pack(fr, first, start, limits(rng, fr))
def setup_inputs_ties(rng):
    fr, first, start = parts(rng); x = fr.reshape(N, 8, 16, W)
    x[:, ::2] = (4096 * rng.integers(-1, 2, (N, 4, 16, W))).astype(np.float32).astype(BF)
    x[..., 0] = 0; x[..., W - 1] = 0; x[..., 5] = -x[..., 7]
    first[:, 0] = W - 1; first[:, W - 1] = 0; first[:, 5] = 7; start[::2, 15::32] = 0; start[::2, 14::32] = 5
    lim = limits(rng, fr); lim[::2] = np.maximum(lim[::2] - rng.integers(0, 2, (4, 16, D)), 0)
    lim[::2, 15] = 0; lim[::2, 14, 0] = 0
    s = cols(fr, start[:, :16]) + cols(fr, np.take_along_axis(first, start[:, :16], 1)); en = np.sum(np.abs(s), axis=(0, 2))
    lim[1::2, :, 0] = np.maximum(en - (np.arange(16) & 1), 0)[1::2]
    return pack(fr, first, start, lim)
def setup_inputs_walls(rng):
    fr, first, start = parts(rng); lim = limits(rng, fr)
    m = ((np.arange(16)[None, :] + rng.integers(0, 16, (8, 1))) % (D + 1))[:, :, None]; lv = np.arange(D)[None, None, :]
    lim = np.where((lv < m) & (rng.random((8, 16, 1)) < 0.6), 2 ** 24 - 1, lim)
    return pack(fr, first, start, np.where(lv == m, 0, lim))
def setup_inputs_alike(rng):
    fr, first, start = parts(rng); lim = limits(rng, fr)
    start[::2] = rng.choice(np.array([0, W - 1, W // 2, 3]), (4, C))
    first[1] = np.arange(W); first[2] = rng.choice(np.array([0, W - 1, W - K, W - K - 1, W - K + 1]), W)
    first[4] = np.where(rng.random(W) < 0.5, W - K, first[4]); first[5] = W - 1 - rng.integers(0, K, W); start[6, ::2] = W - 1
    return pack(fr, first, start, lim)
def setup_inputs_ends(rng):
    fr, first, start = parts(rng); x = fr.reshape(N, 8, 16, W); lv = np.arange(1, D + 1)[None, :]; odd = (np.arange(16) & 1)[:, None]
    x[:, 3] = (32768 * (2 * rng.integers(0, 2, (N, 16, 1)) - 1) * np.where(rng.random(W) < 0.9, 1, -1)).astype(np.float32).astype(BF)
    x[:, 4::3] = np.where(rng.random((N, 2, 16, W)) < 0.5, rng.integers(-255, 256, (N, 2, 16, W)), rng.choice(np.array([-32768, 32768]), (N, 2, 16, W))).astype(np.float32).astype(BF)
    x[:, 5] = rng.integers(-255, 256, (N, 16, W)).astype(np.float32).astype(BF)
    x[int(rng.integers(0, N)), 5] = (32768 * (2 * rng.integers(0, 2, (16, 1)) - 1)).astype(np.float32).astype(BF)
    lim = limits(rng, fr)
    lim[0] = 0; lim[1] = 2 ** 24 - 1; lim[2] = 2 ** 24 - 1; lim[2, :, D - 1] = 0; lim[7, :2] = 2 ** 24 - 1
    lim[3] = 2 ** 21 * (lv + 1) - odd * (lv >= 4)
    lim[5] = 2 ** 19 * (lv + 1) + 2 ** 17
    lim[5, ::2, 3] = rng.integers(2 ** 21 + 2 ** 17, 5 * 2 ** 19, 8)
    if D > 4: lim[5, 1::2, 4] = rng.integers(2 ** 21 + 2 ** 17, 6 * 2 ** 19, 8)
    s = cols(fr, start) + cols(fr, np.take_along_axis(first, start, 1)); sh = np.sum(np.abs(s[:, 4]), axis=1)
    hi = sh.astype(np.float32).astype(BF).astype(np.float64); lo = (sh - hi).astype(np.float32).astype(BF).astype(np.float64); er = np.sum(hi + lo - sh, axis=0)
    for i in range(16):
        c = i + 16 * int(np.argmin(er[i::16]) if i & 1 else np.argmax(er[i::16]))
        lim[4, i, 0] = np.sum(sh[:, c]) - (i & 1)
    return pack(fr, first, start, lim)
def setup_inputs_spread(rng):
    fr, first, start = parts(rng); fr = ints(wide(rng, N, 128, W).astype(np.float32) * 32)
    return pack(fr, first, start, limits(rng, fr))
def check_inputs(d):
    bad = []; v = np.asarray(d["frag"]).astype(np.float32)
    if not np.all((np.abs(v) <= 32768) & (np.rint(v) == v)): bad.append("frag: whole numbers from -32768 to 32768")
    for k, hi in (("first", W - 1), ("start", W - 1), ("lim", 2 ** 24 - 1)):
        if np.min(d[k]) < 0 or np.max(d[k]) > hi: bad.append("range of " + k)
        if np.any(d[k] != d[k][:1]): bad.append(k + " is not alike on all ranks")
    return bad
def reference(frag, first, start, lim):
    fr = frag.astype(np.float32).astype(np.int32).reshape(N, 8, 16, W).transpose(1, 3, 0, 2).reshape(8, W, 16 * N)
    fi = first[0].astype(np.int64); lm = lim[0].astype(np.int64).reshape(8, 16, D)
    M = 8 * C; a = np.arange(M); g = np.repeat(np.arange(8), C); cl = np.tile(np.arange(C) & 15, 8)
    V = np.zeros((M, D + 1), np.int64); Q = np.zeros((M, D + 1), np.int64); S = np.zeros((M, D + 1, 16 * N), np.int32); d = np.zeros(M, np.int64)
    V[:, 0] = gentries(start[0]).reshape(-1); S[:, 0] = fr[g, V[:, 0]]
    for rnd in range(R):
        v = V[a, d]; b = Q[a, d]; live = d < D
        w = (fi[g, v] + K * b) & (W - 1)
        s = S[a, d] + fr[g, w]; en = np.sum(np.abs(s), axis=1); up = np.minimum(d + 1, D)
        go = live & (b < B) & (en <= lm[g, cl, up - 1]); no = live & (b < B) & ~go
        back = live & (b == B) & (d > 0); anew = live & (b == B) & (d == 0)
        Q[a[no], d[no]] += 1
        Q[a[anew], 0] = 0
        Q[a[back], d[back] - 1] += 1
        V[a[go], up[go]] = w[go]; Q[a[go], up[go]] = 0; S[a[go], up[go]] = s[go]
        d = d + go.astype(np.int64) - back.astype(np.int64)
    y = S[a, d].reshape(8, C, N, 16).transpose(2, 0, 3, 1).reshape(N, 128, C)
    t = np.where(np.arange(D + 1)[None, :] <= d[:, None], 16 * V + Q, -1).reshape(8, C, D + 1).transpose(0, 2, 1).reshape(8, -1)
    return {"y": np.ascontiguousarray(y).astype(np.float32), "stk": np.stack([gtable(t)] * N).astype(np.float32)}

from concourse.bass import DstId, RemoteDMATransfer
from concourse.mybir import AluOpType as OP, ActivationFunctionType as AF

W, CH, KC = 8192, 384, 24
WX = W + 2000
FA = 3072
SC = float(2 ** 24)
DEFA = float((64 + 45) << 16)
DEFC = float(((16 + 15) << 19) + 11)
NFV = [1, 0, 0]
CY, GA, PEC, HOP, ISS, FLY, ROW, DL, BW, LOOK, STAG = 1.04e-3, 1.3e-3, 0.5e-3, 0.07, 0.7, 1.5, 0.04, 2.0, 330e3, 0.15, 1.2

F32, I32, U16, B16 = "float32", "int32", "uint16", "bfloat16"
SCRATCH = {
    "FX": ("sbuf", [128, WX], B16), "TB": ("sbuf", [128, WX], B16),
    "FS": ("sbuf", [128, 512], I32), "HI": ("sbuf", [128, 512], B16), "LO": ("sbuf", [128, 512], B16),
    "UU": ("sbuf", [128, 16 * 72], U16), "BH": ("sbuf", [128, 144], B16), "OH": ("sbuf", [128, 8], B16),
    "RG": ("sbuf", [128, 1536], B16), "NG": ("sbuf", [128, 1152], B16),
    "SN": ("sbuf", [128, 20 * 72], F32), "LN": ("sbuf", [128, 15 * 72], F32),
    "FL": ("sbuf", [128, 4, 6, KC], F32), "SK": ("sbuf", [128, 5, 96], F32), "YB": ("sbuf", [128, 1536], F32),
    "QQ": ("sbuf", [128, 4, 2, 96], F32), "MN": ("sbuf", [128, 2, 48], F32), "MX": ("sbuf", [128, 2, 48], F32),
    "K5": ("sbuf", [128, 3, 48], F32), "Q5": ("sbuf", [128, 3, 48], F32), "LT": ("sbuf", [128, 5, 36], I32),
    "PSV": ("psum", [128, 512], F32), "PSN": ("psum", [128, 512], F32), "PSC": ("psum", [128, 512], F32),
}
for _n, _w, _d in [("JI CI CC S2 VM VP EQ XT X3", 24, F32), ("XX XC SO TT DD CP MA MC ML", 24, I32), ("YY ZZ LS DF", 48, F32),
                   ("KA KK T1 EE", 72, F32), ("MW", 72, I32), ("BP M4 SM PN", 96, F32), ("BE STI PJ", 96, I32),
                   ("YL XI B2X", 144, F32), ("LV AA A3 KP F1 SL KQ", 120, F32), ("ST TI XL XB V6 PR", 120, I32),
                   ("US U10 U11 UY", 96, U16), ("L1", 12, U16), ("L3", 36, U16), ("LI PI", 4, I32), ("PF LF", 4, F32),
                   ("OB", 8, F32), ("LR LC", 288, F32), ("SE", 128, F32), ("MK RR GI", 576, F32)]:
    for _k in _n.split():
        SCRATCH[_k] = ("sbuf", [128, _w], _d)
for _k in ("A2", "B2", "C2", "W2"):
    SCRATCH[_k] = ("sbuf", [128, 2, KC], F32)
for _k, _d in (("SY", F32), ("N5", F32), ("I5", I32)):
    SCRATCH[_k] = ("sbuf", [128, 3, KC], _d)
for _q in range(4):
    SCRATCH["SW%d" % _q] = ("sbuf", [128, 16 * CH], F32)
    SCRATCH["SB%d" % _q] = ("sbuf", [128, CH], F32)
    SCRATCH["AB%d" % _q] = ("sbuf", [128, 3 * CH], F32)
    SCRATCH["PE%d" % _q] = ("psum", [128, 512], F32)

SEMAPHORES = (["qv", "qs", "qt", "qg", "ls", "d_first", "d_start", "d_lim", "d_fa", "d_fb", "d_hi", "d_lo", "d_sa", "d_sb"]
              + ["d_y%d" % q for q in range(4)] + ["rs%d" % p for p in range(1, 6)]
              + ["ag%d_%d" % (p, q) for p in range(1, 7) for q in range(4)])
V, S, P, G, Y = "v", "s", "t", "g", "y"
PLAN = {}


def bits(es):
    m = 0
    for e in es:
        m |= 1 << e
    return m


def build(g, r, T, topo):
    core = T.cores[r]
    ops, wr, rd = [], {}, {}
    sh, an = OP.logical_shift_right, OP.bitwise_and

    def op(q, fn, reads, writes, c, dma=None, out=()):
        deps = [wr[k] for k in reads if k in wr]
        for k in writes:
            deps += ([wr[k]] if k in wr else []) + rd.get(k, [])
        me = len(ops)
        ops.append({"q": q, "fn": fn, "deps": deps, "dma": dma, "c": c, "out": list(out), "name": (list(writes) + list(reads))[0]})
        tok = ("x", dma, 16) if dma else ("o", me)
        if q != G or writes:
            for k in reads:
                rd.setdefault(k, []).append(tok)
        for k in writes:
            wr[k] = tok
            rd[k] = []

    def landed(key, sem, val):
        wr[key] = ("x", sem, val)

    def ts(out, in0, s1, s2, o0, o1, reads, writes, n=KC):
        if o1 is None:
            op(V, lambda: g.vector.tensor_scalar(out, in0, s1, None, o0), reads, writes, max(64, n) * CY)
        else:
            op(V, lambda: g.vector.tensor_scalar(out, in0, s1, s2, o0, o1), reads, writes, max(64, n) * CY)

    def tt(out, a, b, o, reads, writes, n=2 * KC):
        op(V, lambda: g.vector.tensor_tensor(out, a, b, o), reads, writes, max(64, n) * CY)

    def cp(out, a, reads, writes, n=KC):
        op(V, lambda: g.vector.tensor_copy(out, a), reads, writes, max(64, n) * CY)

    def fill(ap, c, writes, n=KC):
        op(V, lambda: g.vector.memset(ap, c), [], writes, max(64, n) * CY)

    def act(out, a, f, reads, writes, n):
        op(S, lambda: g.scalar.activation(out, a, f), reads, writes, max(64, n) * CY + 0.03)

    def addc(out, a, c, reads, writes):
        op(S, lambda: g.scalar.activation(out, a, AF.Identity, bias=c), reads, writes, 0.1)

    def gathered(n):
        return int((0.06 + n * GA) / CY)

    def gather(vec, out, a, reads, writes, n):
        if vec:
            cp(out, a, reads, writes, gathered(n))
        else:
            act(out, a, AF.Copy, reads, writes, gathered(n))

    def dma(q, out, a, sem, reads, writes, t):
        e = g.sync if q == Y else g.scalar
        op(q, lambda: e.dma_start(out, a), reads, writes, 0.05, dma=sem, out=[(r, sem, DL + t / BW)])

    def iota(out, pat, cm, writes, n, flag=True):
        if flag:
            op(G, lambda: g.iota(out, pat, 0, cm, allow_small_or_imprecise_dtypes=True), [], writes, 0.13 + 2 * n * CY)
        else:
            op(G, lambda: g.iota(out, pat, 0, cm), [], writes, 0.13 + 2 * n * CY)

    def lv(buf, a, b=None):
        return buf[:, KC * a:KC * (a + 1 if b is None else b)]

    def sums(out, o0, src, c0, ones, reads, writes, k):
        def fn():
            last = None
            for t in range(3):
                last = g.tensor.matmul(out[:, o0 + 8 * t:o0 + 8 * t + 8], src[:, c0 + 128 * t:c0 + 128 * t + 128], ones, True, True)
            return last
        op(P, fn, reads, writes, 3 * 64 * k * PEC)

    def turn(src, n, reads):
        w = KC * n
        tt(T.RR[:, 0:8 * w], src.indirect(T.L1[:] if n == 1 else T.L3[:]), T.MK[:, 0:8 * w], OP.mult,
           reads + ["MK", "L%d" % n], ["RR"], gathered(8 * w))

        def fn():
            last = None
            for x in range(8):
                last = g.tensor.matmul(T.PSC[32 * (x // 2):32 * (x // 2) + 32, 0:w], T.B2X[:, 16 - 16 * (x % 2):48 - 16 * (x % 2)],
                                       T.RR[:, w * x:w * x + w], x % 2 == 0, x % 2 == 1)
            return last
        op(P, fn, ["RR", "B2X"], ["PSC"], 8 * max(32, w) * 4 * PEC)

    peers = [q for q in range(4) if q != r]
    far = [q for q in peers if topo.chip(T.cores[q]) != topo.chip(core)]
    near = [q for q in peers if q not in far]
    fe = topo.engines(core, T.cores[far[0]])
    ne = [e for e in topo.engines(core, T.cores[near[0]]) if e not in fe]
    h = len(fe) // 2
    agm = {far[0]: bits(fe[:h]), far[1]: bits(fe[h:]), near[0]: bits(ne[:h])}
    nls = [0]

    def spread(src, p, reads):
        def fn():
            tr = []
            for q in peers:
                rid, pid, _se = topo.addr(T.cores[q])
                tr.append(RemoteDMATransfer(dst_ids=[DstId(rid=rid, pnc=pid)], dma_engine_mask=agm[q],
                                            remote_sem=T.sem["ag%d_%d" % (p, r)], src=src, dst=src))
            return g.remote_dma_fused(tr, local_sem=T.sem.ls)
        op(G, fn, reads, [], ISS, out=[(q, "ag%d_%d" % (p, r), FLY + 128 // h * ROW) for q in peers])
        nls[0] += 3 * h

    dma(Y, T.FS[:], T.first[:], "d_first", [], ["FS"], 262144)
    dma(Y, T.STI[:], T.start[:], "d_start", [], ["STI"], 311296)
    dma(Y, T.LI[:], T.lim[:], "d_lim", [], ["LI"], 320000)
    dma(Y, T.FX[:, 0:FA], T.frag[:, 0:FA], "d_fa", [], ["FXa"], 320000 + 256 * FA)
    iota(T.PI[:, 0:1], [[0, 1]], 1, ["PI0"], 1, False)
    iota(T.XI[:], [[1, 144]], 0, ["XI"], 144)
    iota(T.JI[:], [[16, KC]], 1, ["JI"], KC)
    iota(T.TB[:, 7168:8192], [[0, 1024]], 0, ["Z4"], 1024)
    iota(T.CC[:], [[128, 3], [0, 8]], 1, ["CC"], KC)
    iota(T.GI[:], [[0, 72], [1, 8]], 0, ["GI"], 576)
    iota(T.SE[:], [[0, 8], [1, 16]], 0, ["SE"], 128)
    iota(T.LT[:, 0, :], [[16, 36]], 1, ["LT0"], 36, False)
    fill(T.TB[:, 0:1024], 0.0, ["Z0"], 512)
    fill(T.TB[:, 1024:4096], 0.0, ["Z1"], 1536)
    for j in range(3):
        act(T.TB[:, 4096 + 1024 * j:5120 + 1024 * j], T.TB[:, 0:1024], AF.Copy, ["Z0"], ["Z2%d" % j], 1024)
    cp(T.HI[:], T.FS[:], ["FS"], ["HI"], 512)
    tt(T.LO[:], T.FS[:], T.HI[:], OP.subtract, ["FS", "HI"], ["LO"], 1024)
    zs = ["Z0", "Z1", "Z20", "Z21", "Z22", "Z4"]
    dma(Y, T.TB[0:128:16, 0:W], T.HI[:], "d_hi", ["HI"] + zs, ["TBh"], 131072)
    dma(Y, T.TB[1:128:16, 0:W], T.LO[:], "d_lo", ["LO"] + zs, ["TBl"], 262144)
    dma(Y, T.FX[:, FA:W], T.frag[:, FA:W], "d_fb", [], ["FXb"], 262144 + 256 * (W - FA))
    cp(T.US[:], T.STI[:], ["STI"], ["US"], 96)
    ts(T.PI[:, 1:2], T.PI[:, 0:1], 4, None, sh, None, ["PI0"], ["PI1"])
    ts(T.LF[:], T.LI[:], SC, None, OP.mult, None, ["LI"], ["LF"])
    ts(T.PF[:, 0:1], T.PI[:, 1:2], 16.0, 15.0, OP.mult, OP.add, ["PI1"], ["PF"])
    cp(T.PF[:, 1:2], T.PI[:, 1:2], ["PI1"], ["PG"])
    ts(T.PF[:, 2:3], T.PI[:, 0:1], T.PF[:, 0:1], 15.0, OP.subtract, OP.add, ["PI0", "PF"], ["PM"])
    ts(T.BH[:], T.XI[:], T.PF[:, 0:1], 8.0, OP.is_equal, OP.mult, ["XI", "PF"], ["BH"], 144)
    ts(T.CI[:], T.JI[:], T.PF[:, 0:1], 15.0, OP.subtract, OP.add, ["JI", "PF"], ["CI"])
    ts(T.OB[:], T.GI[:, 0:8], T.PF[:, 1:2], SC, OP.is_equal, OP.mult, ["GI", "PG"], ["OB"])
    ts(T.OH[:], T.GI[:, 0:8], T.PF[:, 1:2], 8.0, OP.is_equal, OP.mult, ["GI", "PG"], ["OH"])
    ts(T.MK[:], T.GI[:], T.PF[:, 1:2], None, OP.is_equal, None, ["GI", "PG"], ["MK"], 576)
    ts(T.B2X[:, 0:48], T.XI[:, 0:48], 16.0, T.PF[:, 2:3], OP.subtract, OP.is_equal, ["XI", "PM"], ["B2X"])
    ts(T.SE[:], T.SE[:], T.PF[:, 2:3], None, OP.is_equal, None, ["SE", "PM"], ["SE"], 128)
    for l in range(4):
        ts(T.LR[:, 72 * l:72 * l + 72], T.MK[:, 0:72], T.LF[:, l:l + 1], None, OP.mult, None, ["MK", "LF"], ["LR%d" % l], 72)
    op(P, lambda: g.tensor.matmul(T.PSC[:, 0:288], T.SE[:], T.LR[:], True, True), ["SE", "LR0", "LR1", "LR2", "LR3"], ["PSC"], 288 * 4 * PEC)
    cp(T.LC[:], T.PSC[:, 0:288], ["PSC"], ["LC"], 288)
    for l in range(2):
        tt(lv(T.DF, l), T.LC[:, 72 * l + 144:72 * l + 168], T.LC[:, 72 * l + 72:72 * l + 96], OP.subtract, ["LC"], ["LD%d" % l])
    ts(T.LT[:, 0, :], T.LT[:, 0, :], T.PF[:, 0:1], 15.0, OP.subtract, OP.add, ["LT0", "PF"], ["LT0"])
    ts(T.LT[:, 1, :], T.LT[:, 0, :], 3, None, sh, None, ["LT0"], ["LT1"])
    ts(T.LT[:, 4, :], T.LT[:, 1, :], 8.0, None, OP.mult, None, ["LT1"], ["LT4"])
    for nn, mul, bt, L, k in ((3, 43.0, 7, T.L1, 12), (9, 57.0, 9, T.L3, 36)):
        ts(T.LT[:, 2, 0:k], T.LT[:, 1, 0:k], mul, None, OP.mult, None, ["LT1"], ["LT2"])
        ts(T.LT[:, 3, 0:k], T.LT[:, 2, 0:k], bt, None, sh, None, ["LT2"], ["LT3"])
        ts(T.LT[:, 2, 0:k], T.LT[:, 3, 0:k], float(1 - 8 * nn), None, OP.mult, None, ["LT3"], ["LT2"])
        tt(T.LT[:, 3, 0:k], T.LT[:, 2, 0:k], T.LT[:, 4, 0:k], OP.add, ["LT2", "LT4"], ["LT3"])
        cp(L[:], T.LT[:, 3, 0:k], ["LT3"], ["L%d" % (nn // 3)])
    turn(lv(T.STI, r), 1, ["STI"])
    ts(lv(T.ST, 0), T.PSC[:, 0:KC], 32.0, float(15 << 19), OP.mult, OP.add, ["PSC"], ["ST0"])
    fill(T.QQ[:, 0, 0, 72:96], DEFA, ["cA1"])
    fill(T.QQ[:, 0, 1, 72:96], DEFC, ["cC1"])
    fill(lv(T.LV, 0), 1.0, ["LV0"])
    fill(lv(T.KP, 0), 1.0, ["KP0"])
    for b in range(2):
        ts(T.K5[:, 2, KC * b:KC * b + KC], T.CC[:], float(CH * b + 1), None, OP.add, None, ["CC"], ["K52%d" % b])
    act(T.FX[:, W:WX], T.FX[:, 0:WX - W], AF.Copy, ["FXa"], ["FXw"], 2000)
    tb = ["TBh", "TBl"] + zs
    cp(T.TB[:, W:WX], T.TB[:, 0:WX - W], tb, ["TBw"], 1000)
    gather(1, T.RG[:, 0:768], T.TB[:, 0:W].indirect(T.US[:, 0:48]), tb + ["US"], ["RG0"], 768)
    gather(0, T.RG[:, 768:1536], T.TB[:, 0:W].indirect(T.US[:, 48:96]), tb + ["US"], ["RG1"], 768)

    def root():
        last = None
        for i in range(16):
            last = g.tensor.matmul(T.PE0[:, 0:96], T.BH[:, 15 - i:143 - i], T.RG[:, i:1536:16], i == 0, i == 15)
        return last
    op(P, root, ["BH", "RG0", "RG1"], ["PE0"], 16 * 96 * PEC)
    ts(T.U10[:], T.PE0[:, 0:96], 0.125, None, OP.mult, None, ["PE0"], ["U10"], 96)
    ts(T.U11[:], T.PE0[:, 0:96], 0.125, 8.0, OP.mult, OP.add, ["PE0"], ["U11"], 96)
    sums(T.PSN, 0, T.RG, CH * r, T.OH[:], ["OH", "RG0", "RG1"], ["PSN"], 1)
    ts(T.XT[:], T.PSN[:, 0:KC], 4.0, None, OP.mult, None, ["PSN"], ["XT"])
    fx = ["FXa", "FXb", "FXw"]

    def lists(p, q):
        if p == 1:
            return lv(T.U10, q), lv(T.U11, q), None, ["U10", "U11"]
        ks = ["U%d_%d" % (p, q)] if q != r else ["U%d_%d_%d" % (p, q, j) for j in range(3)]
        c = ((p - 2) * 4 + q) * 72
        return T.UU[:, c:c + 24], T.UU[:, c + 24:c + 48], T.UU[:, c + 48:c + 72], ks

    def win(buf, b, u0, u1):
        if b == 0:
            return buf[:, 0:W].indirect(u0)
        if b == 1:
            return buf[:, 992:992 + W + 8].indirect(u1)
        return buf[:, 2000:WX].indirect(u0)

    def slots(q, lo):
        return ["SW%d_%d" % (q, s) for s in range(lo, 16)]

    for p in range(1, 6):
        j = 5 - p
        nb = 3 if p < 5 else 2
        n = KC * nb
        if p < 5:
            u0, u1, u2, uk = lists(p, r)
            for b in range(3):
                gather(NFV[b], T.NG[:, CH * b:CH * b + CH], win(T.TB, b, u0, u1), tb + ["TBw"] + uk, ["NG%d" % b], CH)
                sums(T.PSN, KC * b, T.NG, CH * b, T.OH[:], ["OH", "NG%d" % b], ["PSN"], 1)
        for q in range(4):
            SW, SB, AB, PE = T["SW%d" % q], T["SB%d" % q], T["AB%d" % q], T["PE%d" % q]
            u0, u1, u2, uk = lists(p, q)
            if p == 1:
                base, bk = SW[:, 15 * CH:16 * CH], "SW%d_15" % q
                gather(0, base, T.FX[:, 0:W].indirect(lv(T.US, q)), ["FXa", "FXb", "US"], [bk], CH)
            else:
                base, bk = SB[:], "SB%d" % q
                gather(0, base, SW[:, 3 * (j + 1) * CH:16 * CH].indirect(u2), uk + slots(q, 3 * (j + 1)), [bk], CH)
            for b in range(nb):
                s = 3 * j + b + (1 if p == 5 else 0)
                tt(SW[:, s * CH:s * CH + CH], win(T.FX, b, u0, u1), base, OP.add, fx + uk + [bk], ["SW%d_%d" % (q, s)], gathered(CH))
                act(AB[:, b * CH:b * CH + CH], SW[:, s * CH:s * CH + CH], AF.Abs, ["SW%d_%d" % (q, s)], ["AB%d_%d" % (q, b)], CH)
                sums(PE, KC * b, AB, CH * b, T.OB[:], ["OB", "AB%d_%d" % (q, b)], ["PE%d" % q], 4)
            if q != r:
                c = ((p - 1) * 4 + q) * 72
                act(T.SN[:, c:c + n], PE[:, 0:n], AF.Copy, ["PE%d" % q], ["SN%d_%d" % (p, q)], n)
                d = ((p - 1) * 3 + (r - q - 1) % 4) * 72
                rid, pid, _se = topo.addr(T.cores[q])
                op(G, lambda c=c, d=d, n=n, p=p, rid=rid, pid=pid: g.remote_dma(
                    T.LN[:, d:d + n], T.SN[:, c:c + n], T.sem["rs%d" % p], T.sem.ls, pid, rid, bits(fe)),
                   ["SN%d_%d" % (p, q)], [], ISS, out=[(q, "rs%d" % p, FLY + 128 // len(fe) * ROW)])
                nls[0] += len(fe)
        PE = T["PE%d" % r]
        pe = "PE%d" % r
        ow = ["OW0", "OW1", "OW2"]
        if p < 5:
            if p > 1:
                ts(T.X3[:], T.XC[:], 32.0, None, OP.mult, None, ["XC"], ["X3"])
                tt(T.XT[:], T.X3[:], T.TT[:], OP.add, ["X3", "TT"], ["XT"])
            for b in range(3):
                addc(lv(T.KK, b), T.XT[:], float(((3 * j + b) << 19) + 32000 * b + b + 1), ["XT"], ["KK%d" % b])
            ca = [float((3 * (3 * j + b)) << 16) for b in range(3)]
            if p > 2:
                for b in range(3):
                    ts(lv(T.EE, b), T.DD[:], ca[b] + 1.0, None, OP.add, None, ["DD"], ["EE%d" % b])
                ts(T.X3[:], T.DD[:], float(p - 1), None, OP.is_ge, None, ["DD"], ["X3"])
                tt(lv(T.LS, 0), T.X3[:], lv(T.DF, p - 3), OP.mult, ["X3", "LD%d" % (p - 3)], ["LS0"])
                tt(lv(T.LS, 1), lv(T.LS, 0), T.LC[:, 72 * (p - 2):72 * (p - 2) + KC], OP.add, ["LS0", "LC"], ["LS1"])
                tt(T.KA[:], T.PSN[:, 0:72], T.EE[:], OP.add, ["PSN", "EE0", "EE1", "EE2"], ["KA0", "KA1", "KA2"], 72)
                for b in range(3):
                    tt(lv(T.PSV, b), lv(PE, b), lv(T.LS, 1), OP.subtract, [pe, "LS1"], [ow[b]])
            else:
                for b in range(3):
                    addc(lv(T.KA, b), lv(T.PSN, b), ca[b] + p, ["PSN"], ["KA%d" % b])
                tt(T.PSV[:, 0:72], PE[:, 0:72], T.LC[:, 72 * p - 72:72 * p], OP.subtract, [pe, "LC"], ow, 72)
        else:
            st = ["ST%d" % l for l in range(5)]
            ts(T.TI[:], T.ST[:], 31, None, an, None, st, ["TI"], 120)
            ts(T.V6[:], T.ST[:], 1, 8191 << 4, sh, an, st, ["V6"], 120)
            ts(T.PR[:], T.ST[:], 19, None, sh, None, st, ["PR"], 120)
            ts(T.PJ[:], lv(T.PR, 1, 5), 43.0, None, OP.mult, None, ["PR"], ["PJ"], 96)
            ts(T.BE[:], T.PJ[:], 7, None, sh, None, ["PJ"], ["BE"], 96)
            tt(lv(T.LV, 1, 5), lv(T.TI, 1, 5), lv(T.TI, 0, 4), OP.is_gt, ["TI"], ["LV"], 192)
            ts(T.BP[:], T.BE[:], -3.0, 1.0, OP.mult, OP.add, ["BE"], ["BP"], 96)
            tt(T.BP[:], T.BP[:], lv(T.PR, 1, 5), OP.add, ["BP", "PR"], ["BP"], 192)
            tt(lv(T.M4, 0), lv(T.TI, 1), lv(T.TI, 2), OP.max, ["TI"], ["M40"])
            ts(T.AA[:], T.LV[:], 4.0, None, OP.mult, None, ["LV", "LV0"], ["AA"], 120)
            tt(T.BP[:], T.BP[:], lv(T.LV, 1, 5), OP.mult, ["BP", "LV"], ["BP"], 192)
            ts(lv(T.M4, 1), lv(T.LV, 4), 10.0, None, OP.mult, None, ["LV"], ["M41"])
            tt(lv(T.M4, 2), lv(T.M4, 0), lv(T.TI, 3), OP.max, ["M40", "TI"], ["M42"])
            tt(lv(T.AA, 0, 4), lv(T.AA, 0, 4), T.BP[:], OP.subtract, ["AA", "BP"], ["AA"], 192)
            tt(lv(T.M4, 3), lv(T.M4, 1), lv(T.M4, 2), OP.max, ["M41", "M42"], ["M43"])
            ts(T.A3[:], T.AA[:], -1.0, 3.0, OP.mult, OP.add, ["AA"], ["A3"], 120)
            ts(lv(T.YL, 5), lv(T.M4, 3), -1.0, 14.0, OP.mult, OP.add, ["M43"], ["YL5"])
            for l in (4, 3, 2, 1, 0):
                tt(lv(T.YL, l), lv(T.YL, l + 1), lv(T.AA, l), OP.subtract, ["YL%d" % (l + 1), "AA"], ["YL%d" % l])
            ts(lv(T.PN, 0), T.DD[:], 3.0, 16.0, OP.not_equal, OP.mult, ["DD"], ["PN0"])
            tt(lv(T.PN, 1), lv(T.PN, 0), T.TT[:], OP.add, ["PN0", "TT"], ["PN1"])
            for b in range(2):
                ts(lv(T.PN, 2 + b), lv(T.PN, 1), float(9 - b), float(2 ** 49), OP.is_gt, OP.mult, ["PN1"], ["PN%d" % (2 + b)])
                ts(T.K5[:, 0, KC * b:KC * b + KC], lv(T.V6, 3), b + 1.0, None, OP.add, None, ["V6"], ["K50%d" % b])
            ts(T.K5[:, 1, 0:KC], T.XC[:], 16.0, 1.0, OP.mult, OP.add, ["XC"], ["K510"])
            ts(lv(T.YY, 0), T.XC[:], 16.0, float(16001 + (1 << 18)), OP.mult, OP.add, ["XC"], ["YY1"])
            ts(lv(T.ZZ, 0), T.XC[:], float(W - 1000), -float(1 << 17), OP.is_ge, OP.mult, ["XC"], ["ZZ1"])
            tt(T.K5[:, 1, KC:48], lv(T.YY, 0), lv(T.ZZ, 0), OP.add, ["YY1", "ZZ1"], ["K511"])
            tt(T.XL[:], lv(T.YL, 0, 5), T.A3[:], OP.max, ["YL%d" % l for l in range(5)] + ["A3"], ["XL"], 240)
            ts(lv(T.KP, 1, 5), lv(T.XL, 1, 5), 3.0, None, OP.is_le, None, ["XL"], ["KP"], 96)
            ts(T.XB[:], T.XL[:], 3, None, an, None, ["XL"], ["XB"], 120)
            ts(T.KQ[:], T.KP[:], -100.0, 100.0, OP.mult, OP.add, ["KP", "KP0"], ["KQ"], 120)
            tt(T.F1[:], T.V6[:], T.XB[:], OP.add, ["V6", "XB"], ["F1"], 240)
            tt(T.SL[:], T.PR[:], T.KQ[:], OP.add, ["PR", "KQ"], ["SL"], 240)
            ts(T.F1[:], T.F1[:], 1.0, None, OP.add, None, ["F1"], ["F1"], 120)
            tt(lv(T.SM, 0, 2), lv(T.SL, 0, 2), lv(T.SL, 2, 4), OP.min, ["SL"], ["SM0"], 96)
            tt(T.F1[:], T.F1[:], T.KP[:], OP.mult, ["F1", "KP", "KP0"], ["F1"], 240)
            tt(lv(T.SM, 2), lv(T.SM, 0), lv(T.SM, 1), OP.min, ["SM0"], ["SM2"])
            turn(T.F1[:, 0:72], 3, ["F1"])
            ts(T.FL[:, r, 0:3, :], T.PSC[:, 0:72], -1.0, None, OP.add, None, ["PSC"], ["FLa"], 72)
            spread(T.FL[:, r, 0:3, :], 6, ["FLa"])
            tt(lv(T.SM, 3), lv(T.SM, 2), lv(T.SL, 4), OP.min, ["SM2", "SL"], ["SM3"])
            cp(T.SY[:, 0, :], lv(T.F1, 3), ["F1"], ["SY0"])
            ts(lv(T.SM, 2), lv(T.SM, 3), float(CH), float(1 - CH), OP.mult, OP.add, ["SM3"], ["SM2"])
            ts(T.SY[:, 1, :], lv(T.F1, 4), float(2 << 18), None, OP.add, None, ["F1"], ["SY1"])
            tt(T.SY[:, 2, :], lv(T.SM, 2), T.CC[:], OP.add, ["SM2", "CC"], ["SY2"])
            tt(T.LS[:], PE[:, 0:48], T.LC[:, 216:264], OP.subtract, [pe, "LC"], ["LS0", "LS1"])
            tt(T.PSV[:, 0:48], T.LS[:], lv(T.PN, 2, 4), OP.add, ["LS0", "LS1", "PN2", "PN3"], ow, 96)
        d = (p - 1) * 3 * 72
        landed("LN%d" % p, "rs%d" % p, 3 * len(fe))
        D = T.PSV[:, 144:144 + n]
        tt(T.T1[:, 0:n], T.LN[:, d:d + n], T.LN[:, d + 72:d + 72 + n], OP.add, ["LN%d" % p], ["T1"], 2 * n)
        tt(T.PSV[:, 72:72 + n], T.LN[:, d + 144:d + 144 + n], T.PSV[:, 0:n], OP.add, ["LN%d" % p] + ow, ["T2"], n)
        tt(D, T.T1[:, 0:n], T.PSV[:, 72:72 + n], OP.add, ["T1", "T2"], ["D"], n)
        if p < 5:
            Q = T.QQ
            tt(Q[:, p - 1, 0, 0:72], T.KA[:], D, OP.max, ["D", "KA0", "KA1", "KA2"], ["QA%d" % p], 72)
            tt(T.MN[:, 0, :], Q[:, p - 1, 0, 0:48], Q[:, p - 1, 0, 48:96], OP.min, ["QA%d" % p, "cA%d" % p], ["MNA"], 96)
            tt(T.MA[:], T.MN[:, 0, 0:KC], T.MN[:, 0, KC:48], OP.min, ["MNA"], ["MA"])
            turn(T.MA[:], 1, ["MA"])
            cp(T.ML[:], T.PSC[:, 0:KC], ["PSC"], ["ML"])
            ts(T.SO[:], T.ML[:], 9, 63 << 7, sh, an, ["ML"], ["SO"])
            ts(T.XX[:], T.ML[:], 3, 8191, sh, an, ["ML"], ["XX"])
            ts(T.XC[:], T.MA[:], 3, 8191, sh, an, ["MA"], ["XC"])
            tt(T.S2[:], T.SO[:], T.CI[:], OP.add, ["SO", "CI"], ["S2"])
            u0, u1, u2, uk = lists(p + 1, r)
            cp(u0, T.XX[:], ["XX"], [uk[0]])
            ts(u1, T.XX[:], 8.0, None, OP.add, None, ["XX"], [uk[1]])
            ts(u2, T.S2[:], -float(3 * j * CH), None, OP.add, None, ["S2"], [uk[2]])
            c = ((p - 1) * 4 + r) * 72
            spread(T.UU[:, c:c + 72], p, uk)
        else:
            for k in range(3):
                tt(T.Q5[:, k, :], T.K5[:, k, :], D, OP.max, ["D", "K5%d0" % k, "K5%d1" % k], ["Q5%d" % k])
            tt(T.N5[:], T.Q5[:, :, 0:KC], T.Q5[:, :, KC:48], OP.min, ["Q50", "Q51", "Q52"], ["N5"], 144)
            tt(T.I5[:], T.N5[:], T.SY[:], OP.min, ["N5", "SY0", "SY1", "SY2"], ["I5"], 144)
            ts(T.MW[:], T.I5[:], (1 << 18) - 1, None, an, None, ["I5"], ["MW"], 72)
            turn(T.MW[:], 3, ["MW"])
            ts(T.FL[:, r, 3:6, :], T.PSC[:, 0:72], -1.0, None, OP.add, None, ["PSC"], ["FLb"], 72)
            spread(T.FL[:, r, 3:6, :], p, ["FLb"])
        for q in peers:
            landed("U%d_%d" % (p + 1, q), "ag%d_%d" % (p, q), h)
        if p < 5:
            tt(Q[:, p - 1, 1, 0:72], T.KK[:], D, OP.max, ["D", "KK0", "KK1", "KK2"], ["QC%d" % p], 72)
            ts(T.DD[:], T.MA[:], 7, None, an, None, ["MA"], ["DD"])
            tt(T.MN[:, 1, :], Q[:, p - 1, 1, 0:48], Q[:, p - 1, 1, 48:96], OP.min, ["QC%d" % p, "cC%d" % p], ["MNC"], 96)
            tt(T.MC[:], T.MN[:, 1, 0:KC], T.MN[:, 1, KC:48], OP.min, ["MNC"], ["MC"])
            ts(T.TT[:], T.MC[:], 31, None, an, None, ["MC"], ["TT"])
            node, nk = T.MC[:], "MC"
            if p == 2:
                ts(T.CP[:], node, (1 << 23) - 1, None, an, None, ["MC"], ["CP"])
                node, nk = T.CP[:], "CP"
            ts(T.VM[:], T.TT[:], 10.0, None, OP.is_le, None, ["TT"], ["VM"])
            if p < 4:
                tt(T.MX[:], Q[:, p - 1, :, 0:48], Q[:, p - 1, :, 48:96], OP.max,
                   ["QA%d" % p, "QC%d" % p, "cA%d" % p, "cC%d" % p], ["MX"], 192)
                tt(T.A2[:], T.MN[:, :, 0:KC], T.MN[:, :, KC:48], OP.max, ["MNA", "MNC"], ["A2"], 96)
                tt(T.B2[:], T.MX[:, :, 0:KC], T.MX[:, :, KC:48], OP.min, ["MX"], ["B2"], 96)
                tt(T.C2[:], T.A2[:], T.B2[:], OP.min, ["A2", "B2"], ["C2"], 96)
            if p == 1:
                ts(T.W2[:, 0, :], T.MA[:], float(1 << 22), None, OP.add, None, ["MA"], ["W20"])
                ts(T.W2[:, 1, :], T.MC[:], float((1 << 23) + 4), None, OP.add, None, ["MC"], ["W21"])
                tt(T.C2[:], T.C2[:], T.W2[:], OP.min, ["C2", "W20", "W21"], ["C2"], 96)
                tt(lv(T.ST, 1), T.VM[:], node, OP.mult, ["VM", nk], ["ST1"])
            else:
                ts(T.EQ[:], T.DD[:], float(p), None, OP.is_equal, None, ["DD"], ["EQ"])
                tt(T.VP[:], T.VM[:], node, OP.mult, ["VM", nk], ["VP"])
                for l in {2: [1], 3: [1, 2], 4: [3]}[p]:
                    tt(lv(T.ST, l), lv(T.ST, l), T.VP[:], OP.max, ["ST%d" % l, "VP"], ["ST%d" % l])
                tt(lv(T.ST, p), T.EQ[:], T.VP[:], OP.mult, ["EQ", "VP"], ["ST%d" % p])
            if p < 4:
                ts(Q[:, p, 0, 72:96], T.C2[:, 0, :], DEFA, None, OP.min, None, ["C2"], ["cA%d" % (p + 1)])
                ts(Q[:, p, 1, 72:96], T.C2[:, 1, :], 4.0, DEFC, OP.add, OP.min, ["C2"], ["cC%d" % (p + 1)])

    for q in range(4):
        fa, fb = ["FLa"], ["FLb"]
        if q != r:
            landed("U7_%d" % q, "ag6_%d" % q, h)
            fa, fb = ["U7_%d" % q], ["U6_%d" % q]
        act(T.SK[:, 0:3, KC * q:KC * q + KC], T.FL[:, q, 0:3, :], AF.Copy, fa, ["SKa%d" % q], 72)
        act(T.SK[:, 3:5, KC * q:KC * q + KC], T.FL[:, q, 3:5, :], AF.Copy, fb, ["SKb%d" % q], 48)
        cp(lv(T.UY, q), T.FL[:, q, 5, :], fb, ["UY%d" % q])
        gather(1, T.YB[:, CH * q:CH * q + CH], T["SW%d" % q][:, CH:16 * CH].indirect(lv(T.UY, q)), ["UY%d" % q] + slots(q, 1), ["YB%d" % q], CH)
        dma(Y, T.y[:, CH * q:CH * q + CH], T.YB[:, CH * q:CH * q + CH], "d_y%d" % q, ["YB%d" % q], ["y%d" % q],
            512 * CH + (3 - q) * STAG * BW)
    dma(S, T.stk[:, 0:288], T.SK[:, 0:3, :], "d_sa", ["SKa%d" % q for q in range(4)], ["stka"], 512 * 288)
    dma(S, T.stk[:, 288:480], T.SK[:, 3:5, :], "d_sb", ["SKb%d" % q for q in range(4)], ["stkb"], 512 * 192)
    return ops, nls[0]


def schedule(all_ops):
    cost, prod = {}, {}
    for r in range(4):
        for i, o in enumerate(all_ops[r]):
            cost[r, i] = o["c"]
            for dst, sem, t in o["out"]:
                prod.setdefault((dst, sem), []).append(((r, i), t))
    pred, succ = {}, {k: [] for k in cost}
    for r in range(4):
        lasty = None
        for i, o in enumerate(all_ops[r]):
            e = {}
            for dep in o["deps"]:
                for k, t in ([((r, dep[1]), HOP)] if dep[0] == "o" else prod[r, dep[1]]):
                    e[k] = max(e.get(k, 0.0), t)
            if o["q"] == Y:
                if lasty is not None:
                    e[lasty] = max(e.get(lasty, 0.0), 0.0)
                lasty = (r, i)
            pred[r, i] = e
            for k in e:
                succ[k].append((r, i))
    left = {k: len(succ[k]) for k in cost}
    way, todo = {}, [k for k in cost if left[k] == 0]
    while todo:
        k = todo.pop()
        way[k] = cost[k] + max([pred[s][k] + way[s] for s in succ[k]] + [t for _d, _s, t in all_ops[k[0]][k[1]]["out"]] + [0.0])
        for p in pred[k]:
            left[p] -= 1
            if left[p] == 0:
                todo.append(p)
    for k in way:
        if all_ops[k[0]][k[1]]["name"][:2] == "SN":
            way[k] += 5.0
    left = {k: len(pred[k]) for k in cost}
    free = {(r, q): 0.0 for r in range(4) for q in (V, S, P, G, Y)}
    ready = {k: [] for k in free}
    seq = {k: [] for k in free}
    done = {}
    for k in cost:
        if left[k] == 0:
            ready[k[0], all_ops[k[0]][k[1]]["q"]].append((0.0, k))
    for _n in range(len(cost)):
        e = min((x for x in free if ready[x]), key=lambda x: max(free[x], min(ready[x])[0]))
        t = max(free[e], min(ready[e])[0])
        a = max((x for x in ready[e] if x[0] <= t + LOOK), key=lambda x: (way[x[1]], -x[1][1]))
        ready[e].remove(a)
        k = a[1]
        done[k] = free[e] = max(t, a[0]) + cost[k]
        seq[e].append(k[1])
        for s in succ[k]:
            left[s] -= 1
            if left[s] == 0:
                ready[s[0], all_ops[s[0]][s[1]]["q"]].append((max(done[p] + pred[s][p] for p in pred[s]), s))
    return seq


def rank_program(g, core, T, topo):
    r = T.rank_of(core)
    if r is None:
        return
    if not PLAN:
        PLAN.update(schedule([build(g, q, T, topo)[0] for q in range(4)]))
    ops, nls = build(g, r, T, topo)
    eng = {V: g.vector, S: g.scalar, P: g.tensor, G: g, Y: g.sync}
    qsem = {V: "qv", S: "qs", P: "qt", G: "qg"}
    seq = {q: PLAN[r, q] for q in eng}
    pos = {i: k for q in seq for k, i in enumerate(seq[q])}
    waits, need = {}, set()
    for q in seq:
        seen = {}
        for i in seq[q]:
            want = {}
            for dep in ops[i]["deps"]:
                key, val = (("x", dep[1]), dep[2]) if dep[0] == "x" else (("o", ops[dep[1]]["q"]), pos[dep[1]] + 1)
                if val > seen.get(key, 0) and val > want.get(key, 0):
                    want[key] = val
            waits[i] = sorted(want.items())
            for key, val in waits[i]:
                seen[key] = val
                if key[0] == "o":
                    need.add(seq[key[1]][val - 1])
    count = {}
    for q in seq:
        c = 0
        for i in seq[q]:
            if i in need:
                c += 1
                count[i] = c
    for q in seq:
        for i in seq[q]:
            for key, val in waits[i]:
                if key[0] == "x":
                    eng[q].wait_ge(T.sem[key[1]], val)
                else:
                    eng[q].wait_ge(T.sem[qsem[key[1]]], count[seq[key[1]][val - 1]])
            ins = ops[i]["fn"]()
            if ops[i]["dma"]:
                ins.then_inc(T.sem[ops[i]["dma"]], 16)
            elif i in need:
                ins.then_inc(T.sem[qsem[q]], 1)
    for q in range(4):
        g.sync.wait_ge(T.sem["d_y%d" % q], 16)
    g.scalar.wait_ge(T.sem.d_sa, 16)
    g.scalar.wait_ge(T.sem.d_sb, 16)
    g.wait_ge(T.sem.ls, nls)
